import numpy as np
import ml_dtypes


def mxq(x, axis, fmt="e4m3"):
    dtype, down = {"e4m3": (ml_dtypes.float8_e4m3fn, 7), "e5m2": (ml_dtypes.float8_e5m2, 14)}[fmt]
    v = np.moveaxis(np.asarray(x, np.float32).astype(ml_dtypes.bfloat16).astype(np.float64), axis, -1)
    blocks = v.reshape(v.shape[:-1] + (-1, 32))
    amax = np.abs(blocks).max(-1, keepdims=True)
    byte = np.maximum(np.where(amax > 0, np.frexp(amax)[1] - 1 + 127, 0) - down, 1)
    scale = np.exp2(byte - 127.0)
    codes = (blocks / scale).astype(np.float32).astype(dtype).astype(np.float64)
    return np.moveaxis((codes * scale).reshape(v.shape), -1, axis)


WIDE = False


def mx_kscale(k):
    if not WIDE:
        return np.ones(k)
    levels = np.array([10, -10, 5, -5, 0])
    if k % 512:
        return np.exp2(np.random.permutation(np.resize(levels, k // 32))).repeat(32)
    a = np.empty((k // 512, 16))
    for p in range(k // 512):
        a[p, :8] = np.random.permutation(np.resize(levels, 8))
        for g in range(8):
            far = levels[np.abs(levels - a[p, g]) >= 10]
            a[p, g + 8] = far[np.random.randint(len(far))]
    return np.exp2(a.ravel()).repeat(32)


def f64(x):
    return np.asarray(x).astype(np.float64)


def striped(idx):
    return np.tile(idx.reshape(-1, 16).T, (8, 1)).astype(np.uint16)


def unstriped(offs):
    return offs[:16].T.reshape(-1).astype(np.int64)


def striped8(idx):
    return np.concatenate([x.reshape(-1, 16).T for x in idx]).astype(np.uint16)


def runs(offs, k):
    lists = np.stack([offs[16 * r : 16 * r + 16].T.reshape(-1) for r in range(8)]).astype(np.int64)
    return lists[np.arange(k) % 512 // 64]


def pack_weight(w):
    k, n = w.shape
    w = f64(np.asarray(w, np.float32).astype(ml_dtypes.bfloat16)).reshape(k // 32, 32, n)
    amax = np.abs(w).max(1)
    byte = np.clip(np.where(amax > 0, np.frexp(amax)[1] - 1 + 127 - 7, 1), 1, 254)
    scaled = (w * np.exp2(127.0 - byte)[:, None, :]).reshape(k, n).astype(np.float32)
    words = np.ascontiguousarray(scaled.reshape(k // 512, 128, 4, n).transpose(0, 1, 3, 2)).astype(ml_dtypes.float8_e4m3fn).view(np.uint8)
    return words, np.ascontiguousarray(byte.astype(np.uint8).reshape(k // 512, 16, n))


def unpack_weight(words, scales):
    g, p, n, _ = words.shape
    vals = np.ascontiguousarray(words).view(ml_dtypes.float8_e4m3fn).astype(np.float64) * np.repeat(np.exp2(scales.astype(np.float64) - 127.0), 8, axis=1)[..., None]
    return vals.transpose(0, 1, 3, 2).reshape(g * 512, n)


K, T, S, N, H = 512, 2048, 512, 512, 512


def setup_inputs():
    n = np.random.standard_normal
    s = mx_kscale(K)[:, None]
    u = mx_kscale(S)
    packed_xT = pack_weight(n((K, T)) * s)
    return {
        "x_words": packed_xT[0],
        "x_scales": packed_xT[1],
        "wa": (n((K, H)) / np.sqrt(K) / s).astype(np.float32),
        "wb": (n((K, H)) / np.sqrt(K) / s).astype(np.float32),
        "gt": (np.random.uniform(0.5, 1.5, (S, 1)) * u[:, None]).astype(np.float32),
        "w1": (n((S, N)) / np.sqrt(S) / u[:, None]).astype(np.float32),
        "offs": striped(np.random.permutation(T)[:S]),
        "two": striped(np.random.permutation(T)[:S]),
        "n1": striped8(np.stack([np.random.permutation(H) for _ in range(8)])),
        "n2": striped8(np.stack([np.random.permutation(H) for _ in range(8)])),
        "n3": striped8(np.stack([np.random.permutation(H) for _ in range(8)])),
        "n4": striped8(np.stack([np.random.permutation(H) for _ in range(8)])),
    }


def reference(x_words, x_scales, wa, wb, gt, w1, offs, two, n1, n2, n3, n4):
    xq = unpack_weight(x_words, x_scales)[:, unstriped(offs)]
    y = xq.T @ mxq(f64(wa), 0, "e4m3")
    x_two = unpack_weight(x_words, x_scales)[:, unstriped(two)]
    d = x_two.T @ mxq(f64(wb), 0, "e4m3")
    z = f64(gt) * (0.75 * (y * (d[np.arange(S)[:, None], runs(n2, S)]) - ((y[np.arange(S)[:, None], runs(n1, S)]) * d)))
    h = mxq(f64(w1), 0, "e4m3").T @ mxq(z, 0, "e4m3")
    pa = h[np.arange(N)[:, None], runs(n3, N)]
    pb = h[np.arange(N)[:, None], runs(n4, N)]
    mu = 0.3125 * (h + pa + pb)
    return (h - mu) / (np.sqrt((pa - mu) ** 2 + (pb - mu) ** 2 + 0.25))

@@ -1,0 +1,258 @@
+import math
+from contextlib import ExitStack
+
+import concourse.mybir as mybir
+from concourse.masks import make_identity
+
+K, T, S, N, H = 512, 2048, 512, 512, 512
+FLOPS = 2 * K * S * H * 2 + 2 * S * N * H
+
+F32 = mybir.dt.float32
+BF16 = mybir.dt.bfloat16
+I32 = mybir.dt.int32
+U32 = mybir.dt.uint32
+U16 = mybir.dt.uint16
+U8 = mybir.dt.uint8
+FP8X4 = mybir.dt.float8_e4m3fn_x4
+ALU = mybir.AluOpType
+ACT = mybir.ActivationFunctionType
+
+P = 128
+PACK = 4
+HALF = 256
+Z_CHUNKS = ((0, 256), (256, 384), (384, 512))
+
+
+def tile_picked_twtcrossbstd_none_p_kernel(tc, x_words, x_scales, wa, wb, gt, w1, offs, two, n1, n2, n3, n4, out):
+    nc = tc.nc
+    with ExitStack() as ctx:
+        keep = ctx.enter_context(tc.tile_pool(name="keep", bufs=1))
+        ring = ctx.enter_context(tc.tile_pool(name="ring", bufs=4))
+        psum = ctx.enter_context(tc.psum_pool(name="psum", bufs=2))
+        psum_h = ctx.enter_context(tc.psum_pool(name="psum_h", bufs=1))
+
+        def load_list(src, name):
+            lst = keep.tile([P, S // 16], U16, name=name)
+            nc.sync.dma_start(lst[:], src)
+            return lst
+
+        def load_rows(w, c0, c1, name):
+            raw = keep.tile([P, PACK, c1 - c0], F32, name=name)
+            nc.sync.dma_start(out=raw[:], in_=w.rearrange("(p j) c -> p j c", j=PACK)[:, :, c0:c1])
+            return raw
+
+        scale_table = keep.tile([P, T], U8, name="scale_table", align_bytes=64)
+        nc.vector.memset(scale_table[:].bitcast(I32), 0)
+        for q in range(4):
+            nc.scalar.dma_start(
+                out=scale_table[32 * q : 32 * q + 4, :].bitcast(I32),
+                in_=x_scales[0, 4 * q : 4 * q + 4, :].bitcast(I32),
+            )
+        sixteen = keep.tile([P, 1], F32, name="sixteen")
+        nc.vector.memset(sixteen[:], 16.0)
+        quarter = keep.tile([P, 1], F32, name="quarter")
+        nc.scalar.activation(quarter[:], sixteen[:], ACT.Abs_reciprocal_sqrt)
+
+        offs_list = load_list(offs, "offs_list")
+        word_table = keep.tile([P, T], U32, name="word_table", align_bytes=64)
+        nc.sync.dma_start(
+            out=word_table[:].bitcast(I32),
+            in_=x_words[0].rearrange("p c r -> p (c r)").bitcast(I32),
+        )
+        two_list = load_list(two, "two_list")
+        wa_raw = [load_rows(wa, HALF * i, HALF * (i + 1), f"wa_raw{i}") for i in range(2)]
+        wb_raw = [load_rows(wb, HALF * i, HALF * (i + 1), f"wb_raw{i}") for i in range(2)]
+        gains = keep.tile([P, PACK], F32, name="gains")
+        nc.sync.dma_start(out=gains[:], in_=gt.rearrange("(p t) o -> p (t o)", t=PACK))
+        n2_list = load_list(n2, "n2_list")
+        n1_list = load_list(n1, "n1_list")
+        w1_raw = load_rows(w1, 0, N, "w1_raw")
+        n3_list = load_list(n3, "n3_list")
+        n4_list = load_list(n4, "n4_list")
+        identity = keep.tile([P, P], F32, name="identity")
+        make_identity(nc, identity[:])
+
+        def pick_scales(lst, name):
+            picked = keep.tile([P, S], U8, name=name + "_picked", align_bytes=64)
+            nc.vector.tensor_copy(picked[:], scale_table[:].indirect(lst[:]))
+            dealt = keep.tile([P, PACK, P], U8, name=name + "_dealt", align_bytes=64)
+            nc.vector.tensor_copy(
+                dealt[:].rearrange("p t m -> p m t"), picked[:].rearrange("p (m t) -> p m t", t=PACK)
+            )
+            return dealt
+
+        def pick_words(lst, name):
+            dealt = keep.tile([P, PACK, P], U32, name=name, align_bytes=64)
+            nc.vector.tensor_copy(dealt[:].rearrange("p t m -> p m t"), word_table[:].indirect(lst[:]))
+            return dealt
+
+        xa_scales = pick_scales(offs_list, "xa_scales")
+        xb_scales = pick_scales(two_list, "xb_scales")
+        xa_words = pick_words(offs_list, "xa_words")
+        xb_words = pick_words(two_list, "xb_words")
+
+        def interleave(copy, raw, name):
+            width = raw.shape[2]
+            grouped = keep.tile([P, width, PACK], BF16, name=name, align_bytes=64)
+            copy(
+                grouped[:].rearrange("p (c i) j -> p c j i", i=4),
+                raw[:].rearrange("p j (c i) -> p c j i", i=4),
+            )
+            return grouped
+
+        def quantize(grouped, codes, scales):
+            nc.vector.quantize_mx(
+                out=codes.bitcast(FP8X4), scales=scales, in_=grouped[:].rearrange("p c j -> p (c j)")
+            )
+
+        def mx_tiles(name):
+            codes = keep.tile([P, H], U32, name=name + "_codes", align_bytes=64)
+            scales = keep.tile([P, H], U8, name=name + "_scales", align_bytes=64)
+            return codes, scales
+
+        wa_codes, wa_scales = mx_tiles("wa")
+        wb_codes, wb_scales = mx_tiles("wb")
+        halves = [slice(HALF * i, HALF * (i + 1)) for i in range(2)]
+        wa_bf = [interleave(nc.scalar.copy, wa_raw[i], f"wa_bf{i}") for i in range(2)]
+        wb_bf = [
+            interleave(nc.scalar.copy, wb_raw[0], "wb_bf0"),
+            interleave(nc.vector.tensor_copy, wb_raw[1], "wb_bf1"),
+        ]
+        for i in range(2):
+            quantize(wa_bf[i], wa_codes[:, halves[i]], wa_scales[:, halves[i]])
+        for i in range(2):
+            quantize(wb_bf[i], wb_codes[:, halves[i]], wb_scales[:, halves[i]])
+
+        def product(acc, lhs_codes, lhs_scales, rhs_codes, rhs_scales):
+            nc.tensor.matmul_mx(
+                out=acc,
+                lhsT=lhs_codes.bitcast(FP8X4),
+                lhsT_scale=lhs_scales,
+                rhs=rhs_codes.bitcast(FP8X4),
+                rhs_scale=rhs_scales,
+                start=True,
+                stop=True,
+            )
+
+        y_rows, d_rows = [], []
+        for t in range(PACK):
+            y_acc = psum.tile([P, H], F32, name="y_acc", tag="wide")
+            product(y_acc[:], xa_words[:, t, :], xa_scales[:, t, :], wa_codes[:], wa_scales[:])
+            y_t = keep.tile([P, H], F32, name=f"y_rows{t}")
+            nc.scalar.activation(y_t[:], y_acc[:], ACT.Copy, scale=gains[:, t : t + 1])
+            d_acc = psum.tile([P, H], F32, name="d_acc", tag="other")
+            product(d_acc[:], xb_words[:, t, :], xb_scales[:, t, :], wb_codes[:], wb_scales[:])
+            d_t = keep.tile([P, H], F32, name=f"d_rows{t}")
+            nc.scalar.activation(d_t[:], d_acc[:], ACT.Copy, scale=0.75)
+            y_rows.append(y_t)
+            d_rows.append(d_t)
+
+        w1_bf = keep.tile([P, PACK, P, PACK], BF16, name="w1_bf", align_bytes=64)
+        nc.scalar.copy(
+            w1_bf[:].rearrange("p t m j -> p m j t"), w1_raw[:].rearrange("p j (m t) -> p m j t", t=PACK)
+        )
+        w1_codes, w1_scales = mx_tiles("w1")
+
+        z_codes, z_scales = mx_tiles("z")
+        h_acc = [psum_h.tile([P, H], F32, name=f"h_acc{t}") for t in range(PACK)]
+        h_rows = [keep.tile([P, H], F32, name=f"h_rows{t}") for t in range(PACK)]
+        h_neg = [keep.tile([P, H], F32, name=f"h_neg{t}") for t in range(PACK)]
+        first = keep.tile([P, PACK, H], F32, name="first")
+        second = keep.tile([P, PACK, H], F32, name="second")
+        for t in range(PACK):
+            for i in range(2):
+                entries = slice(HALF * i // 16, HALF * (i + 1) // 16)
+                nc.vector.tensor_tensor(
+                    second[:, t, halves[i]],
+                    y_rows[t][:].indirect(n1_list[:, entries]),
+                    d_rows[t][:, halves[i]],
+                    ALU.mult,
+                )
+                nc.vector.tensor_tensor(
+                    first[:, t, halves[i]],
+                    d_rows[t][:].indirect(n2_list[:, entries]),
+                    y_rows[t][:, halves[i]],
+                    ALU.mult,
+                )
+        nc.vector.quantize_mx(
+            out=w1_codes[:].bitcast(FP8X4),
+            scales=w1_scales[:],
+            in_=w1_bf[:].rearrange("p t m j -> p (t m j)"),
+        )
+        for c0, c1 in Z_CHUNKS:
+            width = c1 - c0
+            z_bf = keep.tile([P, width, PACK], BF16, name=f"z_bf{c0}", align_bytes=64)
+            nc.vector.tensor_tensor(
+                z_bf[:].rearrange("p (c i) t -> p c t i", i=4),
+                first[:, :, c0:c1].rearrange("p t (c i) -> p c t i", i=4),
+                second[:, :, c0:c1].rearrange("p t (c i) -> p c t i", i=4),
+                ALU.subtract,
+            )
+            quantize(z_bf, z_codes[:, c0:c1], z_scales[:, c0:c1])
+            for t in range(PACK):
+                cols = slice(P * t, P * (t + 1))
+                product(
+                    h_acc[t][:, c0:c1], w1_codes[:, cols], w1_scales[:, cols], z_codes[:, c0:c1], z_scales[:, c0:c1]
+                )
+            for t in range(PACK):
+                nc.scalar.copy(h_rows[t][:, c0:c1], h_acc[t][:, c0:c1])
+                nc.scalar.activation(h_neg[t][:, c0:c1], h_acc[t][:, c0:c1], ACT.Copy, scale=-5.0 / 3.0)
+
+        out_rows = out.rearrange("(p t) n -> p t n", t=PACK)
+        blocks = [slice(P * b, P * (b + 1)) for b in range(HALF // P)]
+
+        def add_transposed(acc, parts):
+            for i, part in enumerate(parts):
+                nc.tensor.matmul(
+                    acc, part, identity[:], start=(i == 0), stop=(i == len(parts) - 1), is_transpose=True
+                )
+
+        def fetch(t, i):
+            entries = slice(HALF * i // 16, HALF * (i + 1) // 16)
+            pa_neg = ring.tile([P, HALF], F32, name="pa_neg")
+            nc.vector.tensor_scalar(
+                pa_neg[:], h_rows[t][:].indirect(n3_list[:, entries]), -1.0, 0.0, ALU.mult, ALU.add
+            )
+            return pa_neg
+
+        def fetch_sum(t, i, pa_neg):
+            entries = slice(HALF * i // 16, HALF * (i + 1) // 16)
+            both = ring.tile([P, HALF], F32, name="both")
+            nc.vector.tensor_tensor(both[:], h_rows[t][:].indirect(n4_list[:, entries]), pa_neg[:], ALU.subtract)
+            return both
+
+        def forms(t, i, pa_neg, both):
+            gap = ring.tile([P, HALF], F32, name="gap")
+            nc.vector.scalar_tensor_tensor(gap[:], pa_neg[:], 2.0, both[:], ALU.mult, ALU.add)
+            top = ring.tile([P, HALF], F32, name="top")
+            nc.vector.scalar_tensor_tensor(top[:], h_neg[t][:, halves[i]], 1.32, both[:], ALU.mult, ALU.add)
+            turned = psum.tile([P, 2, HALF], F32, name="turned", tag="wide")
+            for b in blocks:
+                add_transposed(turned[:, 0, b], [both[:, b], h_neg[t][:, halves[i]][:, b]])
+            for b in blocks:
+                add_transposed(turned[:, 1, b], [gap[:, b]])
+            squares = ring.tile([P, 2, HALF], F32, name="squares")
+            nc.scalar.activation(squares[:, 0, :], turned[:, 0, :], ACT.Square, scale=0.375 * math.sqrt(0.5))
+            nc.scalar.activation(squares[:, 1, :], turned[:, 1, :], ACT.Square, scale=math.sqrt(0.5))
+            spread = psum.tile([P, HALF], F32, name="spread", tag="other")
+            for b in blocks:
+                add_transposed(spread[:, b], [squares[:, 0, b], squares[:, 1, b]])
+            inverse = ring.tile([P, HALF], F32, name="inverse")
+            nc.scalar.activation(inverse[:], spread[:], ACT.Abs_reciprocal_sqrt, bias=quarter[:])
+            return top, inverse
+
+        def finish(t, i, top, inverse):
+            result = ring.tile([P, HALF], F32, name="result")
+            nc.vector.scalar_tensor_tensor(result[:], top[:], -0.3125, inverse[:], ALU.mult, ALU.mult)
+            nc.sync.dma_start(out=out_rows[:, t, halves[i]], in_=result[:])
+
+        pending = []
+        for t in range(PACK):
+            negs = [fetch(t, i) for i in range(2)]
+            sums = [fetch_sum(t, i, negs[i]) for i in range(2)]
+            done = [forms(t, i, negs[i], sums[i]) for i in range(2)]
+            for tt, i, top, inverse in pending:
+                finish(tt, i, top, inverse)
+            pending = [(t, i) + done[i] for i in range(2)]
+        for tt, i, top, inverse in pending:
+            finish(tt, i, top, inverse)

@@ -20,7 +20,8 @@ ACT = mybir.ActivationFunctionType
 P = 128
 PACK = 4
 HALF = 256
-Z_CHUNKS = ((0, 256), (256, 384), (384, 512))
+WA_PIECES = (slice(0, 256), slice(256, 512))
+WB_PIECES = (slice(0, 256), slice(256, 384), slice(384, 512))
 
 
 def tile_picked_twtcrossbstd_none_p_kernel(tc, x_words, x_scales, wa, wb, gt, w1, offs, two, n1, n2, n3, n4, out):
@@ -36,15 +37,16 @@ def tile_picked_twtcrossbstd_none_p_kernel(tc, x_words, x_scales, wa, wb, gt, w1
             nc.sync.dma_start(lst[:], src)
             return lst
 
-        def load_rows(w, c0, c1, name):
-            raw = keep.tile([P, PACK, c1 - c0], F32, name=name)
-            nc.sync.dma_start(out=raw[:], in_=w.rearrange("(p j) c -> p j c", j=PACK)[:, :, c0:c1])
+        def load_rows(w, cols, name):
+            raw = keep.tile([P, PACK, cols.stop - cols.start], F32, name=name, tag=name, align_bytes=64)
+            nc.sync.dma_start(out=raw[:], in_=w.rearrange("(p j) c -> p j c", j=PACK)[:, :, cols])
             return raw
 
         scale_table = keep.tile([P, T], U8, name="scale_table", align_bytes=64)
-        nc.vector.memset(scale_table[:].bitcast(I32), 0)
+        nc.vector.memset(scale_table[:, : T // 2].bitcast(I32), 0)
+        nc.gpsimd.memset(scale_table[:, T // 2 :].bitcast(I32), 0)
         for q in range(4):
-            nc.scalar.dma_start(
+            nc.sync.dma_start(
                 out=scale_table[32 * q : 32 * q + 4, :].bitcast(I32),
                 in_=x_scales[0, 4 * q : 4 * q + 4, :].bitcast(I32),
             )
@@ -54,19 +56,27 @@ def tile_picked_twtcrossbstd_none_p_kernel(tc, x_words, x_scales, wa, wb, gt, w1
         nc.scalar.activation(quarter[:], sixteen[:], ACT.Abs_reciprocal_sqrt)
 
         offs_list = load_list(offs, "offs_list")
+        two_list = load_list(two, "two_list")
         word_table = keep.tile([P, T], U32, name="word_table", align_bytes=64)
         nc.sync.dma_start(
             out=word_table[:].bitcast(I32),
             in_=x_words[0].rearrange("p c r -> p (c r)").bitcast(I32),
         )
-        two_list = load_list(two, "two_list")
-        wa_raw = [load_rows(wa, HALF * i, HALF * (i + 1), f"wa_raw{i}") for i in range(2)]
-        wb_raw = [load_rows(wb, HALF * i, HALF * (i + 1), f"wb_raw{i}") for i in range(2)]
-        gains = keep.tile([P, PACK], F32, name="gains")
-        nc.sync.dma_start(out=gains[:], in_=gt.rearrange("(p t) o -> p (t o)", t=PACK))
-        n2_list = load_list(n2, "n2_list")
+        wa_raw = [load_rows(wa, cols, f"wa_raw{cols.start}") for cols in WA_PIECES]
+        wb_raw = [load_rows(wb, cols, f"wb_raw{cols.start}") for cols in WB_PIECES]
         n1_list = load_list(n1, "n1_list")
-        w1_raw = load_rows(w1, 0, N, "w1_raw")
+        n2_list = load_list(n2, "n2_list")
+        gains = keep.tile([P, PACK], F32, name="gains")
+        w1_raw = keep.tile([P, PACK, N], F32, name="w1_raw")
+        with nc.allow_non_contiguous_dma(reason="one gain for each place"):
+            for s in range(PACK):
+                nc.sync.dma_start(
+                    out=gains[s:P:PACK, :], in_=gt[:, 0].rearrange("(r t s) -> s r t", t=PACK, s=PACK)[s]
+                )
+        for s in range(PACK):
+            nc.sync.dma_start(
+                out=w1_raw[s:P:PACK, :, :], in_=w1.rearrange("(r t s) c -> s r t c", t=PACK, s=PACK)[s]
+            )
         n3_list = load_list(n3, "n3_list")
         n4_list = load_list(n4, "n4_list")
         identity = keep.tile([P, P], F32, name="identity")
@@ -77,51 +87,47 @@ def tile_picked_twtcrossbstd_none_p_kernel(tc, x_words, x_scales, wa, wb, gt, w1
             nc.vector.tensor_copy(picked[:], scale_table[:].indirect(lst[:]))
             dealt = keep.tile([P, PACK, P], U8, name=name + "_dealt", align_bytes=64)
             nc.vector.tensor_copy(
-                dealt[:].rearrange("p t m -> p m t"), picked[:].rearrange("p (m t) -> p m t", t=PACK)
+                dealt[:].rearrange("p t m -> p (t m)").bitcast(I32).rearrange("p (t r) -> p t r", t=PACK),
+                picked[:].bitcast(I32).rearrange("p (r t) -> p t r", t=PACK),
             )
             return dealt
 
         def pick_words(lst, name):
             dealt = keep.tile([P, PACK, P], U32, name=name, align_bytes=64)
-            nc.vector.tensor_copy(dealt[:].rearrange("p t m -> p m t"), word_table[:].indirect(lst[:]))
+            nc.vector.tensor_copy(dealt[:].rearrange("p t (r s) -> p r t s", s=PACK), word_table[:].indirect(lst[:]))
             return dealt
 
-        xa_scales = pick_scales(offs_list, "xa_scales")
-        xb_scales = pick_scales(two_list, "xb_scales")
         xa_words = pick_words(offs_list, "xa_words")
         xb_words = pick_words(two_list, "xb_words")
+        xa_scales = pick_scales(offs_list, "xa_scales")
+        xb_scales = pick_scales(two_list, "xb_scales")
 
-        def interleave(copy, raw, name):
-            width = raw.shape[2]
-            grouped = keep.tile([P, width, PACK], BF16, name=name, align_bytes=64)
-            copy(
-                grouped[:].rearrange("p (c i) j -> p c j i", i=4),
-                raw[:].rearrange("p j (c i) -> p c j i", i=4),
-            )
-            return grouped
+        halves = [slice(HALF * i, HALF * (i + 1)) for i in range(2)]
+        whole = slice(0, H)
 
-        def quantize(grouped, codes, scales):
-            nc.vector.quantize_mx(
-                out=codes.bitcast(FP8X4), scales=scales, in_=grouped[:].rearrange("p c j -> p (c j)")
-            )
+        def round_weights(raws, pieces, copies, name):
+            grouped = keep.tile([P, H, PACK], BF16, name=name, tag=name, align_bytes=64)
+            for raw, cols, copy in zip(raws, pieces, copies):
+                copy(
+                    grouped[:, cols, :].rearrange("p (c i) j -> p c j i", i=4),
+                    raw[:].rearrange("p j (c i) -> p c j i", i=4),
+                )
+            return grouped[:].rearrange("p c j -> p (c j)")
+
+        def quantize(values, codes, scales):
+            nc.vector.quantize_mx(out=codes.bitcast(FP8X4), scales=scales, in_=values)
 
         def mx_tiles(name):
             codes = keep.tile([P, H], U32, name=name + "_codes", align_bytes=64)
             scales = keep.tile([P, H], U8, name=name + "_scales", align_bytes=64)
             return codes, scales
 
-        wa_codes, wa_scales = mx_tiles("wa")
         wb_codes, wb_scales = mx_tiles("wb")
-        halves = [slice(HALF * i, HALF * (i + 1)) for i in range(2)]
-        wa_bf = [interleave(nc.scalar.copy, wa_raw[i], f"wa_bf{i}") for i in range(2)]
-        wb_bf = [
-            interleave(nc.scalar.copy, wb_raw[0], "wb_bf0"),
-            interleave(nc.vector.tensor_copy, wb_raw[1], "wb_bf1"),
-        ]
-        for i in range(2):
-            quantize(wa_bf[i], wa_codes[:, halves[i]], wa_scales[:, halves[i]])
-        for i in range(2):
-            quantize(wb_bf[i], wb_codes[:, halves[i]], wb_scales[:, halves[i]])
+        wa_bf = round_weights(wa_raw, WA_PIECES, [nc.scalar.copy] * 2, "wa_bf")
+        wa_codes, wa_scales = mx_tiles("wa")
+        quantize(wa_bf, wa_codes[:], wa_scales[:])
+        wb_bf = round_weights(wb_raw, WB_PIECES, [nc.scalar.copy] + [nc.vector.tensor_copy] * 2, "wb_bf")
+        quantize(wb_bf, wb_codes[:], wb_scales[:])
 
         def product(acc, lhs_codes, lhs_scales, rhs_codes, rhs_scales):
             nc.tensor.matmul_mx(
@@ -135,124 +141,143 @@ def tile_picked_twtcrossbstd_none_p_kernel(tc, x_words, x_scales, wa, wb, gt, w1
             )
 
         y_rows, d_rows = [], []
+        d_banks = [(psum_h, "rows2"), (psum_h, "rows3"), (psum, "wide"), (psum, "other"), (psum, "wide")]
         for t in range(PACK):
-            y_acc = psum.tile([P, H], F32, name="y_acc", tag="wide")
+            y_acc = psum_h.tile([P, H], F32, name=f"y_acc{t}", tag=f"rows{t}")
             product(y_acc[:], xa_words[:, t, :], xa_scales[:, t, :], wa_codes[:], wa_scales[:])
             y_t = keep.tile([P, H], F32, name=f"y_rows{t}")
-            nc.scalar.activation(y_t[:], y_acc[:], ACT.Copy, scale=gains[:, t : t + 1])
-            d_acc = psum.tile([P, H], F32, name="d_acc", tag="other")
-            product(d_acc[:], xb_words[:, t, :], xb_scales[:, t, :], wb_codes[:], wb_scales[:])
+            nc.scalar.activation(y_t[:], y_acc[:], ACT.Copy, scale=0.75)
             d_t = keep.tile([P, H], F32, name=f"d_rows{t}")
-            nc.scalar.activation(d_t[:], d_acc[:], ACT.Copy, scale=0.75)
+            for cols in halves if t == 0 else [whole]:
+                pool, tag = d_banks.pop(0)
+                d_acc = pool.tile([P, cols.stop - cols.start], F32, name="d_acc", tag=tag)
+                product(d_acc[:], xb_words[:, t, :], xb_scales[:, t, :], wb_codes[:, cols], wb_scales[:, cols])
+                nc.scalar.activation(d_t[:, cols], d_acc[:], ACT.Copy, scale=gains[:, t : t + 1])
             y_rows.append(y_t)
             d_rows.append(d_t)
 
-        w1_bf = keep.tile([P, PACK, P, PACK], BF16, name="w1_bf", align_bytes=64)
+        w1_bf = keep.tile([P, PACK, P, PACK], BF16, name="w1_bf", tag="w1_bf", align_bytes=64)
         nc.scalar.copy(
             w1_bf[:].rearrange("p t m j -> p m j t"), w1_raw[:].rearrange("p j (m t) -> p m j t", t=PACK)
         )
         w1_codes, w1_scales = mx_tiles("w1")
 
         z_codes, z_scales = mx_tiles("z")
-        h_acc = [psum_h.tile([P, H], F32, name=f"h_acc{t}") for t in range(PACK)]
-        h_rows = [keep.tile([P, H], F32, name=f"h_rows{t}") for t in range(PACK)]
-        h_neg = [keep.tile([P, H], F32, name=f"h_neg{t}") for t in range(PACK)]
-        first = keep.tile([P, PACK, H], F32, name="first")
-        second = keep.tile([P, PACK, H], F32, name="second")
-        for t in range(PACK):
-            for i in range(2):
-                entries = slice(HALF * i // 16, HALF * (i + 1) // 16)
+        h_acc = [psum_h.tile([P, H], F32, name=f"h_acc{t}", tag=f"rows{t}") for t in range(PACK)]
+        h_rows = [keep.tile([P, 2 * H], F32, name=f"h_rows{t}") for t in range(PACK)]
+        h_far = [keep.tile([P, H], F32, name=f"h_far{t}") for t in range(PACK)]
+
+        def entries(cols):
+            return slice(cols.start // 16, cols.stop // 16)
+
+        def crossed(cols, tag):
+            both = keep.tile([P, 2, PACK, HALF], F32, name="both", tag=tag, align_bytes=64)
+            first, second = both[:, 0], both[:, 1]
+            for t in range(PACK):
                 nc.vector.tensor_tensor(
-                    second[:, t, halves[i]],
-                    y_rows[t][:].indirect(n1_list[:, entries]),
-                    d_rows[t][:, halves[i]],
-                    ALU.mult,
+                    second[:, t, :], y_rows[t][:].indirect(n1_list[:, entries(cols)]), d_rows[t][:, cols], ALU.mult
                 )
                 nc.vector.tensor_tensor(
-                    first[:, t, halves[i]],
-                    d_rows[t][:].indirect(n2_list[:, entries]),
-                    y_rows[t][:, halves[i]],
-                    ALU.mult,
+                    first[:, t, :], d_rows[t][:].indirect(n2_list[:, entries(cols)]), y_rows[t][:, cols], ALU.mult
                 )
-        nc.vector.quantize_mx(
-            out=w1_codes[:].bitcast(FP8X4),
-            scales=w1_scales[:],
-            in_=w1_bf[:].rearrange("p t m j -> p (t m j)"),
-        )
-        for c0, c1 in Z_CHUNKS:
-            width = c1 - c0
-            z_bf = keep.tile([P, width, PACK], BF16, name=f"z_bf{c0}", align_bytes=64)
+            return first, second
+
+        def round_z(first, second, part):
+            z_bf = keep.tile([P, part.stop - part.start, PACK], BF16, name="z_bf", align_bytes=64, bufs=3)
             nc.vector.tensor_tensor(
                 z_bf[:].rearrange("p (c i) t -> p c t i", i=4),
-                first[:, :, c0:c1].rearrange("p t (c i) -> p c t i", i=4),
-                second[:, :, c0:c1].rearrange("p t (c i) -> p c t i", i=4),
+                first[:, :, part].rearrange("p t (c i) -> p c t i", i=4),
+                second[:, :, part].rearrange("p t (c i) -> p c t i", i=4),
                 ALU.subtract,
             )
-            quantize(z_bf, z_codes[:, c0:c1], z_scales[:, c0:c1])
+            return z_bf[:].rearrange("p c t -> p (c t)")
+
+        def mix(z_bf, cols):
+            quantize(z_bf, z_codes[:, cols], z_scales[:, cols])
             for t in range(PACK):
-                cols = slice(P * t, P * (t + 1))
-                product(
-                    h_acc[t][:, c0:c1], w1_codes[:, cols], w1_scales[:, cols], z_codes[:, c0:c1], z_scales[:, c0:c1]
-                )
-            for t in range(PACK):
-                nc.scalar.copy(h_rows[t][:, c0:c1], h_acc[t][:, c0:c1])
-                nc.scalar.activation(h_neg[t][:, c0:c1], h_acc[t][:, c0:c1], ACT.Copy, scale=-5.0 / 3.0)
+                places = slice(P * t, P * (t + 1))
+                product(h_acc[t][:, cols], w1_codes[:, places], w1_scales[:, places], z_codes[:, cols], z_scales[:, cols])
+
+        def copy_h(t, cols):
+            nc.scalar.copy(h_rows[t][:, cols], h_acc[t][:, cols])
+            nc.scalar.activation(
+                h_rows[t][:, H + cols.start : H + cols.stop], h_acc[t][:, cols], ACT.Copy, scale=8.0 / 15.0
+            )
+            nc.scalar.activation(h_far[t][:, cols], h_acc[t][:, cols], ACT.Copy, scale=2.2)
+
+        first, second = crossed(halves[0], "left")
+        z_left = round_z(first, second, slice(0, HALF))
+        quantize(w1_bf[:].rearrange("p t m j -> p (t m j)"), w1_codes[:], w1_scales[:])
+        mix(z_left, halves[0])
+        for t in range(PACK):
+            copy_h(t, halves[0])
+        first, second = crossed(halves[1], "w1_bf")
+        quarters = [slice(0, P), slice(P, HALF)]
+        z_right = [round_z(first, second, part) for part in quarters]
+        for z_bf, part in zip(z_right, quarters):
+            mix(z_bf, slice(HALF + part.start, HALF + part.stop))
+        for t in range(PACK):
+            copy_h(t, halves[1])
 
         out_rows = out.rearrange("(p t) n -> p t n", t=PACK)
-        blocks = [slice(P * b, P * (b + 1)) for b in range(HALF // P)]
+        lead = [keep.tile([P, H], F32, name=f"lead{t}") for t in range(PACK)]
+        top = [keep.tile([P, H], F32, name=f"top{t}") for t in range(PACK)]
+        gap = [keep.tile([P, H], F32, name=f"gap{t}") for t in range(PACK)]
+        inverse = [keep.tile([P, H], F32, name=f"inverse{t}") for t in range(PACK)]
 
         def add_transposed(acc, parts):
-            for i, part in enumerate(parts):
-                nc.tensor.matmul(
-                    acc, part, identity[:], start=(i == 0), stop=(i == len(parts) - 1), is_transpose=True
+            for b in range(acc.shape[1] // P):
+                block = slice(P * b, P * (b + 1))
+                for i, part in enumerate(parts):
+                    nc.tensor.matmul(
+                        acc[:, block],
+                        part[:, block],
+                        identity[:],
+                        start=(i == 0),
+                        stop=(i == len(parts) - 1),
+                        is_transpose=True,
+                    )
+
+        def fetch(pieces, banks):
+            for t, cols in pieces:
+                nc.vector.tensor_tensor(
+                    lead[t][:, cols], h_rows[t][:].indirect(n3_list[:, entries(cols)]), h_far[t][:, cols], ALU.subtract
                 )
+            for t, cols in pieces:
+                nc.vector.tensor_tensor(
+                    top[t][:, cols], h_rows[t][:].indirect(n4_list[:, entries(cols)]), lead[t][:, cols], ALU.add
+                )
+            for t, cols in pieces:
+                nc.vector.scalar_tensor_tensor(
+                    gap[t][:, cols], lead[t][:, cols], 2.0, top[t][:, cols], ALU.mult, ALU.subtract
+                )
+            squares = []
+            for t, cols in pieces:
+                width = cols.stop - cols.start
+                pair = ring.tile([P, 2, width], F32, name="pair")
+                along = psum.tile([P, width], F32, name="along", tag="wide")
+                add_transposed(along[:], [top[t][:, cols], h_rows[t][:, H + cols.start : H + cols.stop]])
+                nc.scalar.activation(pair[:, 0, :], along[:], ACT.Square, scale=0.375 * math.sqrt(0.5))
+                squares.append(pair)
+            for (t, cols), pair in zip(pieces, squares):
+                across = psum.tile([P, cols.stop - cols.start], F32, name="across", tag="other")
+                add_transposed(across[:], [gap[t][:, cols], h_far[t][:, cols]])
+                nc.scalar.activation(pair[:, 1, :], across[:], ACT.Square, scale=math.sqrt(0.5))
+            for (t, cols), pair, bank in zip(pieces, squares, banks):
+                spread = psum_h.tile([P, cols.stop - cols.start], F32, name="spread", tag=bank)
+                add_transposed(spread[:], [pair[:, 0, :], pair[:, 1, :]])
+                nc.scalar.activation(inverse[t][:, cols], spread[:], ACT.Abs_reciprocal_sqrt, bias=quarter[:])
 
-        def fetch(t, i):
-            entries = slice(HALF * i // 16, HALF * (i + 1) // 16)
-            pa_neg = ring.tile([P, HALF], F32, name="pa_neg")
-            nc.vector.tensor_scalar(
-                pa_neg[:], h_rows[t][:].indirect(n3_list[:, entries]), -1.0, 0.0, ALU.mult, ALU.add
-            )
-            return pa_neg
+        def finish(t, cols):
+            result = ring.tile([P, cols.stop - cols.start], F32, name="result")
+            nc.vector.scalar_tensor_tensor(result[:], top[t][:, cols], -0.3125, inverse[t][:, cols], ALU.mult, ALU.mult)
+            nc.sync.dma_start(out=out_rows[:, t, cols], in_=result[:])
 
-        def fetch_sum(t, i, pa_neg):
-            entries = slice(HALF * i // 16, HALF * (i + 1) // 16)
-            both = ring.tile([P, HALF], F32, name="both")
-            nc.vector.tensor_tensor(both[:], h_rows[t][:].indirect(n4_list[:, entries]), pa_neg[:], ALU.subtract)
-            return both
-
-        def forms(t, i, pa_neg, both):
-            gap = ring.tile([P, HALF], F32, name="gap")
-            nc.vector.scalar_tensor_tensor(gap[:], pa_neg[:], 2.0, both[:], ALU.mult, ALU.add)
-            top = ring.tile([P, HALF], F32, name="top")
-            nc.vector.scalar_tensor_tensor(top[:], h_neg[t][:, halves[i]], 1.32, both[:], ALU.mult, ALU.add)
-            turned = psum.tile([P, 2, HALF], F32, name="turned", tag="wide")
-            for b in blocks:
-                add_transposed(turned[:, 0, b], [both[:, b], h_neg[t][:, halves[i]][:, b]])
-            for b in blocks:
-                add_transposed(turned[:, 1, b], [gap[:, b]])
-            squares = ring.tile([P, 2, HALF], F32, name="squares")
-            nc.scalar.activation(squares[:, 0, :], turned[:, 0, :], ACT.Square, scale=0.375 * math.sqrt(0.5))
-            nc.scalar.activation(squares[:, 1, :], turned[:, 1, :], ACT.Square, scale=math.sqrt(0.5))
-            spread = psum.tile([P, HALF], F32, name="spread", tag="other")
-            for b in blocks:
-                add_transposed(spread[:, b], [squares[:, 0, b], squares[:, 1, b]])
-            inverse = ring.tile([P, HALF], F32, name="inverse")
-            nc.scalar.activation(inverse[:], spread[:], ACT.Abs_reciprocal_sqrt, bias=quarter[:])
-            return top, inverse
-
-        def finish(t, i, top, inverse):
-            result = ring.tile([P, HALF], F32, name="result")
-            nc.vector.scalar_tensor_tensor(result[:], top[:], -0.3125, inverse[:], ALU.mult, ALU.mult)
-            nc.sync.dma_start(out=out_rows[:, t, halves[i]], in_=result[:])
-
-        pending = []
-        for t in range(PACK):
-            negs = [fetch(t, i) for i in range(2)]
-            sums = [fetch_sum(t, i, negs[i]) for i in range(2)]
-            done = [forms(t, i, negs[i], sums[i]) for i in range(2)]
-            for tt, i, top, inverse in pending:
-                finish(tt, i, top, inverse)
-            pending = [(t, i) + done[i] for i in range(2)]
-        for tt, i, top, inverse in pending:
-            finish(tt, i, top, inverse)
+        fetch([(0, halves[0]), (0, halves[1])], ["rows0", "rows1"])
+        fetch([(1, whole), (2, whole)], ["rows2", "rows3"])
+        finish(0, whole)
+        fetch([(3, halves[0]), (3, halves[1])], ["rows0", "rows1"])
+        finish(1, whole)
+        finish(2, whole)
+        finish(3, halves[0])
+        finish(3, halves[1])

@@ -127,7 +127,8 @@ def tile_picked_twtcrossbstd_none_p_kernel(tc, x_words, x_scales, wa, wb, gt, w1
         wa_codes, wa_scales = mx_tiles("wa")
         quantize(wa_bf, wa_codes[:], wa_scales[:])
         wb_bf = round_weights(wb_raw, WB_PIECES, [nc.scalar.copy] + [nc.vector.tensor_copy] * 2, "wb_bf")
-        quantize(wb_bf, wb_codes[:], wb_scales[:])
+        for cols in halves:
+            quantize(wb_bf[:, PACK * cols.start : PACK * cols.stop], wb_codes[:, cols], wb_scales[:, cols])
 
         def product(acc, lhs_codes, lhs_scales, rhs_codes, rhs_scales):
             nc.tensor.matmul_mx(
@@ -164,8 +165,8 @@ def tile_picked_twtcrossbstd_none_p_kernel(tc, x_words, x_scales, wa, wb, gt, w1
 
         z_codes, z_scales = mx_tiles("z")
         h_acc = [psum_h.tile([P, H], F32, name=f"h_acc{t}", tag=f"rows{t}") for t in range(PACK)]
-        h_rows = [keep.tile([P, 2 * H], F32, name=f"h_rows{t}") for t in range(PACK)]
-        h_far = [keep.tile([P, H], F32, name=f"h_far{t}") for t in range(PACK)]
+        h_rows = [keep.tile([P, H], F32, name=f"h_rows{t}") for t in range(PACK)]
+        h_neg = [keep.tile([P, H], F32, name=f"h_neg{t}") for t in range(PACK)]
 
         def entries(cols):
             return slice(cols.start // 16, cols.stop // 16)
@@ -192,41 +193,42 @@ def tile_picked_twtcrossbstd_none_p_kernel(tc, x_words, x_scales, wa, wb, gt, w1
             )
             return z_bf[:].rearrange("p c t -> p (c t)")
 
-        def mix(z_bf, cols):
-            quantize(z_bf, z_codes[:, cols], z_scales[:, cols])
+        def mix(parts):
             for t in range(PACK):
                 places = slice(P * t, P * (t + 1))
-                product(h_acc[t][:, cols], w1_codes[:, places], w1_scales[:, places], z_codes[:, cols], z_scales[:, cols])
+                for cols in parts:
+                    product(
+                        h_acc[t][:, cols], w1_codes[:, places], w1_scales[:, places], z_codes[:, cols], z_scales[:, cols]
+                    )
 
-        def copy_h(t, cols):
-            nc.scalar.copy(h_rows[t][:, cols], h_acc[t][:, cols])
-            nc.scalar.activation(
-                h_rows[t][:, H + cols.start : H + cols.stop], h_acc[t][:, cols], ACT.Copy, scale=8.0 / 15.0
-            )
-            nc.scalar.activation(h_far[t][:, cols], h_acc[t][:, cols], ACT.Copy, scale=2.2)
+        def copy_h(cols):
+            for t in range(PACK):
+                nc.scalar.copy(h_rows[t][:, cols], h_acc[t][:, cols])
+                nc.scalar.activation(h_neg[t][:, cols], h_acc[t][:, cols], ACT.Copy, scale=-5.0 / 3.0)
 
         first, second = crossed(halves[0], "left")
         z_left = round_z(first, second, slice(0, HALF))
         quantize(w1_bf[:].rearrange("p t m j -> p (t m j)"), w1_codes[:], w1_scales[:])
-        mix(z_left, halves[0])
-        for t in range(PACK):
-            copy_h(t, halves[0])
+        quantize(z_left, z_codes[:, halves[0]], z_scales[:, halves[0]])
+        mix([halves[0]])
+        copy_h(halves[0])
         first, second = crossed(halves[1], "w1_bf")
-        quarters = [slice(0, P), slice(P, HALF)]
-        z_right = [round_z(first, second, part) for part in quarters]
-        for z_bf, part in zip(z_right, quarters):
-            mix(z_bf, slice(HALF + part.start, HALF + part.stop))
-        for t in range(PACK):
-            copy_h(t, halves[1])
+        z_right = [round_z(first, second, slice(P * i, P * (i + 1))) for i in range(2)]
+        quarters = [slice(HALF + P * i, HALF + P * (i + 1)) for i in range(2)]
+        for z_bf, cols in zip(z_right, quarters):
+            quantize(z_bf, z_codes[:, cols], z_scales[:, cols])
+        mix(quarters)
+        copy_h(halves[1])
 
         out_rows = out.rearrange("(p t) n -> p t n", t=PACK)
-        lead = [keep.tile([P, H], F32, name=f"lead{t}") for t in range(PACK)]
-        top = [keep.tile([P, H], F32, name=f"top{t}") for t in range(PACK)]
+        pa_neg = [keep.tile([P, H], F32, name=f"pa_neg{t}") for t in range(PACK)]
+        both = [keep.tile([P, H], F32, name=f"both{t}") for t in range(PACK)]
         gap = [keep.tile([P, H], F32, name=f"gap{t}") for t in range(PACK)]
+        top = [keep.tile([P, H], F32, name=f"top{t}") for t in range(PACK)]
         inverse = [keep.tile([P, H], F32, name=f"inverse{t}") for t in range(PACK)]
 
         def add_transposed(acc, parts):
-            for b in range(acc.shape[1] // P):
+            for b in range(HALF // P):
                 block = slice(P * b, P * (b + 1))
                 for i, part in enumerate(parts):
                     nc.tensor.matmul(
@@ -238,46 +240,51 @@ def tile_picked_twtcrossbstd_none_p_kernel(tc, x_words, x_scales, wa, wb, gt, w1
                         is_transpose=True,
                     )
 
-        def fetch(pieces, banks):
-            for t, cols in pieces:
-                nc.vector.tensor_tensor(
-                    lead[t][:, cols], h_rows[t][:].indirect(n3_list[:, entries(cols)]), h_far[t][:, cols], ALU.subtract
+        def fetch(t):
+            for cols in halves:
+                nc.vector.tensor_scalar(
+                    pa_neg[t][:, cols], h_rows[t][:].indirect(n3_list[:, entries(cols)]), -1.0, 0.0, ALU.mult, ALU.add
                 )
-            for t, cols in pieces:
+            for cols in halves:
                 nc.vector.tensor_tensor(
-                    top[t][:, cols], h_rows[t][:].indirect(n4_list[:, entries(cols)]), lead[t][:, cols], ALU.add
+                    both[t][:, cols], h_rows[t][:].indirect(n4_list[:, entries(cols)]), pa_neg[t][:, cols], ALU.subtract
                 )
-            for t, cols in pieces:
+            for cols in halves:
                 nc.vector.scalar_tensor_tensor(
-                    gap[t][:, cols], lead[t][:, cols], 2.0, top[t][:, cols], ALU.mult, ALU.subtract
+                    gap[t][:, cols], pa_neg[t][:, cols], 2.0, both[t][:, cols], ALU.mult, ALU.add
                 )
-            squares = []
-            for t, cols in pieces:
-                width = cols.stop - cols.start
-                pair = ring.tile([P, 2, width], F32, name="pair")
-                along = psum.tile([P, width], F32, name="along", tag="wide")
-                add_transposed(along[:], [top[t][:, cols], h_rows[t][:, H + cols.start : H + cols.stop]])
+            squares = [ring.tile([P, 2, HALF], F32, name="squares") for cols in halves]
+            for cols, pair in zip(halves, squares):
+                along = psum.tile([P, HALF], F32, name="along", tag="wide")
+                add_transposed(along[:], [both[t][:, cols], h_neg[t][:, cols]])
                 nc.scalar.activation(pair[:, 0, :], along[:], ACT.Square, scale=0.375 * math.sqrt(0.5))
-                squares.append(pair)
-            for (t, cols), pair in zip(pieces, squares):
-                across = psum.tile([P, cols.stop - cols.start], F32, name="across", tag="other")
-                add_transposed(across[:], [gap[t][:, cols], h_far[t][:, cols]])
+            for cols, pair in zip(halves, squares):
+                across = psum.tile([P, HALF], F32, name="across", tag="other")
+                add_transposed(across[:], [gap[t][:, cols]])
                 nc.scalar.activation(pair[:, 1, :], across[:], ACT.Square, scale=math.sqrt(0.5))
-            for (t, cols), pair, bank in zip(pieces, squares, banks):
-                spread = psum_h.tile([P, cols.stop - cols.start], F32, name="spread", tag=bank)
+            for i, (cols, pair) in enumerate(zip(halves, squares)):
+                spread = psum_h.tile([P, HALF], F32, name="spread", tag=f"rows{(2 * t + i) % PACK}")
                 add_transposed(spread[:], [pair[:, 0, :], pair[:, 1, :]])
                 nc.scalar.activation(inverse[t][:, cols], spread[:], ACT.Abs_reciprocal_sqrt, bias=quarter[:])
+
+        def numerator(t):
+            nc.vector.scalar_tensor_tensor(top[t][:], h_neg[t][:], 1.32, both[t][:], ALU.mult, ALU.add)
 
         def finish(t, cols):
             result = ring.tile([P, cols.stop - cols.start], F32, name="result")
             nc.vector.scalar_tensor_tensor(result[:], top[t][:, cols], -0.3125, inverse[t][:, cols], ALU.mult, ALU.mult)
             nc.sync.dma_start(out=out_rows[:, t, cols], in_=result[:])
 
-        fetch([(0, halves[0]), (0, halves[1])], ["rows0", "rows1"])
-        fetch([(1, whole), (2, whole)], ["rows2", "rows3"])
+        fetch(0)
+        fetch(1)
+        numerator(0)
+        fetch(2)
         finish(0, whole)
-        fetch([(3, halves[0]), (3, halves[1])], ["rows0", "rows1"])
+        numerator(1)
+        fetch(3)
+        numerator(2)
         finish(1, whole)
+        numerator(3)
         finish(2, whole)
         finish(3, halves[0])
         finish(3, halves[1])

@@ -20,6 +20,7 @@ ACT = mybir.ActivationFunctionType
 P = 128
 PACK = 4
 HALF = 256
+GAIN_RUN = 13
 WA_PIECES = (slice(0, 256), slice(256, 512))
 WB_PIECES = (slice(0, 256), slice(256, 384), slice(384, 512))
 
@@ -64,15 +65,14 @@ def tile_picked_twtcrossbstd_none_p_kernel(tc, x_words, x_scales, wa, wb, gt, w1
         )
         wa_raw = [load_rows(wa, cols, f"wa_raw{cols.start}") for cols in WA_PIECES]
         wb_raw = [load_rows(wb, cols, f"wb_raw{cols.start}") for cols in WB_PIECES]
+        gains = keep.tile([P, 16], F32, name="gains")
+        w1_raw = keep.tile([P, PACK, N], F32, name="w1_raw")
+        for s in range(PACK):
+            nc.sync.dma_start(
+                out=gains[s:P:PACK, :GAIN_RUN], in_=gt[:, 0].rearrange("(r c) -> r c", c=16)[:, s : s + GAIN_RUN]
+            )
         n1_list = load_list(n1, "n1_list")
         n2_list = load_list(n2, "n2_list")
-        gains = keep.tile([P, PACK], F32, name="gains")
-        w1_raw = keep.tile([P, PACK, N], F32, name="w1_raw")
-        with nc.allow_non_contiguous_dma(reason="one gain for each place"):
-            for s in range(PACK):
-                nc.sync.dma_start(
-                    out=gains[s:P:PACK, :], in_=gt[:, 0].rearrange("(r t s) -> s r t", t=PACK, s=PACK)[s]
-                )
         for s in range(PACK):
             nc.sync.dma_start(
                 out=w1_raw[s:P:PACK, :, :], in_=w1.rearrange("(r t s) c -> s r t c", t=PACK, s=PACK)[s]
@@ -126,7 +126,7 @@ def tile_picked_twtcrossbstd_none_p_kernel(tc, x_words, x_scales, wa, wb, gt, w1
         wa_bf = round_weights(wa_raw, WA_PIECES, [nc.scalar.copy] * 2, "wa_bf")
         wa_codes, wa_scales = mx_tiles("wa")
         quantize(wa_bf, wa_codes[:], wa_scales[:])
-        wb_bf = round_weights(wb_raw, WB_PIECES, [nc.scalar.copy] + [nc.vector.tensor_copy] * 2, "wb_bf")
+        wb_bf = round_weights(wb_raw, WB_PIECES, [nc.scalar.copy] * 2 + [nc.vector.tensor_copy], "wb_bf")
         for cols in halves:
             quantize(wb_bf[:, PACK * cols.start : PACK * cols.stop], wb_codes[:, cols], wb_scales[:, cols])
 
@@ -142,7 +142,7 @@ def tile_picked_twtcrossbstd_none_p_kernel(tc, x_words, x_scales, wa, wb, gt, w1
             )
 
         y_rows, d_rows = [], []
-        d_banks = [(psum_h, "rows2"), (psum_h, "rows3"), (psum, "wide"), (psum, "other"), (psum, "wide")]
+        d_banks = [(psum_h, "rows1"), (psum_h, "rows2"), (psum_h, "rows3"), (psum, "wide"), (psum, "other")]
         for t in range(PACK):
             y_acc = psum_h.tile([P, H], F32, name=f"y_acc{t}", tag=f"rows{t}")
             product(y_acc[:], xa_words[:, t, :], xa_scales[:, t, :], wa_codes[:], wa_scales[:])
@@ -153,13 +153,19 @@ def tile_picked_twtcrossbstd_none_p_kernel(tc, x_words, x_scales, wa, wb, gt, w1
                 pool, tag = d_banks.pop(0)
                 d_acc = pool.tile([P, cols.stop - cols.start], F32, name="d_acc", tag=tag)
                 product(d_acc[:], xb_words[:, t, :], xb_scales[:, t, :], wb_codes[:, cols], wb_scales[:, cols])
-                nc.scalar.activation(d_t[:, cols], d_acc[:], ACT.Copy, scale=gains[:, t : t + 1])
+                if cols == halves[0]:
+                    nc.vector.tensor_scalar(d_t[:, cols], d_acc[:], gains[:, PACK * t : PACK * t + 1], None, ALU.mult)
+                else:
+                    nc.scalar.activation(d_t[:, cols], d_acc[:], ACT.Copy, scale=gains[:, PACK * t : PACK * t + 1])
             y_rows.append(y_t)
             d_rows.append(d_t)
 
-        w1_bf = keep.tile([P, PACK, P, PACK], BF16, name="w1_bf", tag="w1_bf", align_bytes=64)
+        left = keep.tile([P, 2 * PACK * HALF], F32, name="left")
+        right = keep.tile([P, 2 * PACK * HALF], F32, name="right", align_bytes=64)
+        w1_bf = right[:, PACK * HALF :].bitcast(BF16)
         nc.scalar.copy(
-            w1_bf[:].rearrange("p t m j -> p m j t"), w1_raw[:].rearrange("p j (m t) -> p m j t", t=PACK)
+            w1_bf.rearrange("p (t m j) -> p m j t", t=PACK, j=PACK),
+            w1_raw[:].rearrange("p j (m t) -> p m j t", t=PACK),
         )
         w1_codes, w1_scales = mx_tiles("w1")
 
@@ -171,9 +177,9 @@ def tile_picked_twtcrossbstd_none_p_kernel(tc, x_words, x_scales, wa, wb, gt, w1
         def entries(cols):
             return slice(cols.start // 16, cols.stop // 16)
 
-        def crossed(cols, tag):
-            both = keep.tile([P, 2, PACK, HALF], F32, name="both", tag=tag, align_bytes=64)
-            first, second = both[:, 0], both[:, 1]
+        def crossed(cols, products):
+            by_tile = products[:].rearrange("p (t k c) -> p t k c", t=PACK, k=2)
+            first, second = by_tile[:, :, 0, :], by_tile[:, :, 1, :]
             for t in range(PACK):
                 nc.vector.tensor_tensor(
                     second[:, t, :], y_rows[t][:].indirect(n1_list[:, entries(cols)]), d_rows[t][:, cols], ALU.mult
@@ -206,13 +212,13 @@ def tile_picked_twtcrossbstd_none_p_kernel(tc, x_words, x_scales, wa, wb, gt, w1
                 nc.scalar.copy(h_rows[t][:, cols], h_acc[t][:, cols])
                 nc.scalar.activation(h_neg[t][:, cols], h_acc[t][:, cols], ACT.Copy, scale=-5.0 / 3.0)
 
-        first, second = crossed(halves[0], "left")
+        first, second = crossed(halves[0], left)
         z_left = round_z(first, second, slice(0, HALF))
-        quantize(w1_bf[:].rearrange("p t m j -> p (t m j)"), w1_codes[:], w1_scales[:])
+        quantize(w1_bf, w1_codes[:], w1_scales[:])
         quantize(z_left, z_codes[:, halves[0]], z_scales[:, halves[0]])
         mix([halves[0]])
         copy_h(halves[0])
-        first, second = crossed(halves[1], "w1_bf")
+        first, second = crossed(halves[1], right)
         z_right = [round_z(first, second, slice(P * i, P * (i + 1))) for i in range(2)]
         quarters = [slice(HALF + P * i, HALF + P * (i + 1)) for i in range(2)]
         for z_bf, cols in zip(z_right, quarters):

import math
from contextlib import ExitStack

import concourse.mybir as mybir
from concourse.masks import make_identity

K, T, S, N, H = 512, 2048, 512, 512, 512
FLOPS = 2 * K * S * H * 2 + 2 * S * N * H

F32 = mybir.dt.float32
BF16 = mybir.dt.bfloat16
I32 = mybir.dt.int32
U32 = mybir.dt.uint32
U16 = mybir.dt.uint16
U8 = mybir.dt.uint8
FP8X4 = mybir.dt.float8_e4m3fn_x4
ALU = mybir.AluOpType
ACT = mybir.ActivationFunctionType

P = 128
PACK = 4
HALF = 256
GAIN_RUN = 13
WA_PIECES = (slice(0, 256), slice(256, 512))
WB_PIECES = (slice(0, 256), slice(256, 384), slice(384, 512))


def tile_picked_twtcrossbstd_none_p_kernel(tc, x_words, x_scales, wa, wb, gt, w1, offs, two, n1, n2, n3, n4, out):
    nc = tc.nc
    with ExitStack() as ctx:
        keep = ctx.enter_context(tc.tile_pool(name="keep", bufs=1))
        ring = ctx.enter_context(tc.tile_pool(name="ring", bufs=4))
        psum = ctx.enter_context(tc.psum_pool(name="psum", bufs=2))
        psum_h = ctx.enter_context(tc.psum_pool(name="psum_h", bufs=1))

        def load_list(src, name):
            lst = keep.tile([P, S // 16], U16, name=name)
            nc.sync.dma_start(lst[:], src)
            return lst

        def load_rows(w, cols, name):
            raw = keep.tile([P, PACK, cols.stop - cols.start], F32, name=name, tag=name, align_bytes=64)
            nc.sync.dma_start(out=raw[:], in_=w.rearrange("(p j) c -> p j c", j=PACK)[:, :, cols])
            return raw

        scale_table = keep.tile([P, T], U8, name="scale_table", align_bytes=64)
        nc.vector.memset(scale_table[:, : T // 2].bitcast(I32), 0)
        nc.gpsimd.memset(scale_table[:, T // 2 :].bitcast(I32), 0)
        for q in range(4):
            nc.sync.dma_start(
                out=scale_table[32 * q : 32 * q + 4, :].bitcast(I32),
                in_=x_scales[0, 4 * q : 4 * q + 4, :].bitcast(I32),
            )
        sixteen = keep.tile([P, 1], F32, name="sixteen")
        nc.vector.memset(sixteen[:], 16.0)
        quarter = keep.tile([P, 1], F32, name="quarter")
        nc.scalar.activation(quarter[:], sixteen[:], ACT.Abs_reciprocal_sqrt)

        offs_list = load_list(offs, "offs_list")
        two_list = load_list(two, "two_list")
        word_table = keep.tile([P, T], U32, name="word_table", align_bytes=64)
        nc.sync.dma_start(
            out=word_table[:].bitcast(I32),
            in_=x_words[0].rearrange("p c r -> p (c r)").bitcast(I32),
        )
        wa_raw = [load_rows(wa, cols, f"wa_raw{cols.start}") for cols in WA_PIECES]
        wb_raw = [load_rows(wb, cols, f"wb_raw{cols.start}") for cols in WB_PIECES]
        gains = keep.tile([P, 16], F32, name="gains")
        w1_raw = keep.tile([P, PACK, N], F32, name="w1_raw")
        for s in range(PACK):
            nc.sync.dma_start(
                out=gains[s:P:PACK, :GAIN_RUN], in_=gt[:, 0].rearrange("(r c) -> r c", c=16)[:, s : s + GAIN_RUN]
            )
        n1_list = load_list(n1, "n1_list")
        n2_list = load_list(n2, "n2_list")
        for s in range(PACK):
            nc.sync.dma_start(
                out=w1_raw[s:P:PACK, :, :], in_=w1.rearrange("(r t s) c -> s r t c", t=PACK, s=PACK)[s]
            )
        n3_list = load_list(n3, "n3_list")
        n4_list = load_list(n4, "n4_list")
        identity = keep.tile([P, P], F32, name="identity")
        make_identity(nc, identity[:])

        def pick_scales(lst, name):
            picked = keep.tile([P, S], U8, name=name + "_picked", align_bytes=64)
            nc.vector.tensor_copy(picked[:], scale_table[:].indirect(lst[:]))
            dealt = keep.tile([P, PACK, P], U8, name=name + "_dealt", align_bytes=64)
            nc.vector.tensor_copy(
                dealt[:].rearrange("p t m -> p (t m)").bitcast(I32).rearrange("p (t r) -> p t r", t=PACK),
                picked[:].bitcast(I32).rearrange("p (r t) -> p t r", t=PACK),
            )
            return dealt

        def pick_words(lst, name):
            dealt = keep.tile([P, PACK, P], U32, name=name, align_bytes=64)
            nc.vector.tensor_copy(dealt[:].rearrange("p t (r s) -> p r t s", s=PACK), word_table[:].indirect(lst[:]))
            return dealt

        xa_words = pick_words(offs_list, "xa_words")
        xb_words = pick_words(two_list, "xb_words")
        xa_scales = pick_scales(offs_list, "xa_scales")
        xb_scales = pick_scales(two_list, "xb_scales")

        halves = [slice(HALF * i, HALF * (i + 1)) for i in range(2)]
        whole = slice(0, H)

        def round_weights(raws, pieces, copies, name):
            grouped = keep.tile([P, H, PACK], BF16, name=name, tag=name, align_bytes=64)
            for raw, cols, copy in zip(raws, pieces, copies):
                copy(
                    grouped[:, cols, :].rearrange("p (c i) j -> p c j i", i=4),
                    raw[:].rearrange("p j (c i) -> p c j i", i=4),
                )
            return grouped[:].rearrange("p c j -> p (c j)")

        def quantize(values, codes, scales):
            nc.vector.quantize_mx(out=codes.bitcast(FP8X4), scales=scales, in_=values)

        def mx_tiles(name):
            codes = keep.tile([P, H], U32, name=name + "_codes", align_bytes=64)
            scales = keep.tile([P, H], U8, name=name + "_scales", align_bytes=64)
            return codes, scales

        wb_codes, wb_scales = mx_tiles("wb")
        wa_bf = round_weights(wa_raw, WA_PIECES, [nc.scalar.copy] * 2, "wa_bf")
        wa_codes, wa_scales = mx_tiles("wa")
        quantize(wa_bf, wa_codes[:], wa_scales[:])
        wb_bf = round_weights(wb_raw, WB_PIECES, [nc.scalar.copy] * 2 + [nc.vector.tensor_copy], "wb_bf")
        for cols in halves:
            quantize(wb_bf[:, PACK * cols.start : PACK * cols.stop], wb_codes[:, cols], wb_scales[:, cols])

        def product(acc, lhs_codes, lhs_scales, rhs_codes, rhs_scales):
            nc.tensor.matmul_mx(
                out=acc,
                lhsT=lhs_codes.bitcast(FP8X4),
                lhsT_scale=lhs_scales,
                rhs=rhs_codes.bitcast(FP8X4),
                rhs_scale=rhs_scales,
                start=True,
                stop=True,
            )

        y_rows, d_rows = [], []
        d_banks = [(psum_h, "rows1"), (psum_h, "rows2"), (psum_h, "rows3"), (psum, "wide"), (psum, "other")]
        for t in range(PACK):
            y_acc = psum_h.tile([P, H], F32, name=f"y_acc{t}", tag=f"rows{t}")
            product(y_acc[:], xa_words[:, t, :], xa_scales[:, t, :], wa_codes[:], wa_scales[:])
            y_t = keep.tile([P, H], F32, name=f"y_rows{t}")
            nc.scalar.activation(y_t[:], y_acc[:], ACT.Copy, scale=0.75)
            d_t = keep.tile([P, H], F32, name=f"d_rows{t}")
            for cols in halves if t == 0 else [whole]:
                pool, tag = d_banks.pop(0)
                d_acc = pool.tile([P, cols.stop - cols.start], F32, name="d_acc", tag=tag)
                product(d_acc[:], xb_words[:, t, :], xb_scales[:, t, :], wb_codes[:, cols], wb_scales[:, cols])
                if cols == halves[0]:
                    nc.vector.tensor_scalar(d_t[:, cols], d_acc[:], gains[:, PACK * t : PACK * t + 1], None, ALU.mult)
                else:
                    nc.scalar.activation(d_t[:, cols], d_acc[:], ACT.Copy, scale=gains[:, PACK * t : PACK * t + 1])
            y_rows.append(y_t)
            d_rows.append(d_t)

        left = keep.tile([P, 2 * PACK * HALF], F32, name="left")
        right = keep.tile([P, 2 * PACK * HALF], F32, name="right", align_bytes=64)
        w1_bf = right[:, PACK * HALF :].bitcast(BF16)
        nc.scalar.copy(
            w1_bf.rearrange("p (t m j) -> p m j t", t=PACK, j=PACK),
            w1_raw[:].rearrange("p j (m t) -> p m j t", t=PACK),
        )
        w1_codes, w1_scales = mx_tiles("w1")

        z_codes, z_scales = mx_tiles("z")
        h_acc = [psum_h.tile([P, H], F32, name=f"h_acc{t}", tag=f"rows{t}") for t in range(PACK)]
        h_rows = [keep.tile([P, H], F32, name=f"h_rows{t}") for t in range(PACK)]
        h_neg = [keep.tile([P, H], F32, name=f"h_neg{t}") for t in range(PACK)]

        def entries(cols):
            return slice(cols.start // 16, cols.stop // 16)

        def crossed(cols, products):
            by_tile = products[:].rearrange("p (t k c) -> p t k c", t=PACK, k=2)
            first, second = by_tile[:, :, 0, :], by_tile[:, :, 1, :]
            for t in range(PACK):
                nc.vector.tensor_tensor(
                    second[:, t, :], y_rows[t][:].indirect(n1_list[:, entries(cols)]), d_rows[t][:, cols], ALU.mult
                )
                nc.vector.tensor_tensor(
                    first[:, t, :], d_rows[t][:].indirect(n2_list[:, entries(cols)]), y_rows[t][:, cols], ALU.mult
                )
            return first, second

        def round_z(first, second, part):
            z_bf = keep.tile([P, part.stop - part.start, PACK], BF16, name="z_bf", align_bytes=64, bufs=3)
            nc.vector.tensor_tensor(
                z_bf[:].rearrange("p (c i) t -> p c t i", i=4),
                first[:, :, part].rearrange("p t (c i) -> p c t i", i=4),
                second[:, :, part].rearrange("p t (c i) -> p c t i", i=4),
                ALU.subtract,
            )
            return z_bf[:].rearrange("p c t -> p (c t)")

        def mix(parts):
            for t in range(PACK):
                places = slice(P * t, P * (t + 1))
                for cols in parts:
                    product(
                        h_acc[t][:, cols], w1_codes[:, places], w1_scales[:, places], z_codes[:, cols], z_scales[:, cols]
                    )

        def copy_h(cols):
            for t in range(PACK):
                nc.scalar.copy(h_rows[t][:, cols], h_acc[t][:, cols])
                nc.scalar.activation(h_neg[t][:, cols], h_acc[t][:, cols], ACT.Copy, scale=-5.0 / 3.0)

        first, second = crossed(halves[0], left)
        z_left = round_z(first, second, slice(0, HALF))
        quantize(w1_bf, w1_codes[:], w1_scales[:])
        quantize(z_left, z_codes[:, halves[0]], z_scales[:, halves[0]])
        mix([halves[0]])
        copy_h(halves[0])
        first, second = crossed(halves[1], right)
        z_right = [round_z(first, second, slice(P * i, P * (i + 1))) for i in range(2)]
        quarters = [slice(HALF + P * i, HALF + P * (i + 1)) for i in range(2)]
        for z_bf, cols in zip(z_right, quarters):
            quantize(z_bf, z_codes[:, cols], z_scales[:, cols])
        mix(quarters)
        copy_h(halves[1])

        out_rows = out.rearrange("(p t) n -> p t n", t=PACK)
        pa_neg = [keep.tile([P, H], F32, name=f"pa_neg{t}") for t in range(PACK)]
        both = [keep.tile([P, H], F32, name=f"both{t}") for t in range(PACK)]
        gap = [keep.tile([P, H], F32, name=f"gap{t}") for t in range(PACK)]
        top = [keep.tile([P, H], F32, name=f"top{t}") for t in range(PACK)]
        inverse = [keep.tile([P, H], F32, name=f"inverse{t}") for t in range(PACK)]

        def add_transposed(acc, parts):
            for b in range(HALF // P):
                block = slice(P * b, P * (b + 1))
                for i, part in enumerate(parts):
                    nc.tensor.matmul(
                        acc[:, block],
                        part[:, block],
                        identity[:],
                        start=(i == 0),
                        stop=(i == len(parts) - 1),
                        is_transpose=True,
                    )

        def fetch(t):
            for cols in halves:
                nc.vector.tensor_scalar(
                    pa_neg[t][:, cols], h_rows[t][:].indirect(n3_list[:, entries(cols)]), -1.0, 0.0, ALU.mult, ALU.add
                )
            for cols in halves:
                nc.vector.tensor_tensor(
                    both[t][:, cols], h_rows[t][:].indirect(n4_list[:, entries(cols)]), pa_neg[t][:, cols], ALU.subtract
                )
            for cols in halves:
                nc.vector.scalar_tensor_tensor(
                    gap[t][:, cols], pa_neg[t][:, cols], 2.0, both[t][:, cols], ALU.mult, ALU.add
                )
            squares = [ring.tile([P, 2, HALF], F32, name="squares") for cols in halves]
            for cols, pair in zip(halves, squares):
                along = psum.tile([P, HALF], F32, name="along", tag="wide")
                add_transposed(along[:], [both[t][:, cols], h_neg[t][:, cols]])
                nc.scalar.activation(pair[:, 0, :], along[:], ACT.Square, scale=0.375 * math.sqrt(0.5))
            for cols, pair in zip(halves, squares):
                across = psum.tile([P, HALF], F32, name="across", tag="other")
                add_transposed(across[:], [gap[t][:, cols]])
                nc.scalar.activation(pair[:, 1, :], across[:], ACT.Square, scale=math.sqrt(0.5))
            for i, (cols, pair) in enumerate(zip(halves, squares)):
                spread = psum_h.tile([P, HALF], F32, name="spread", tag=f"rows{(2 * t + i) % PACK}")
                add_transposed(spread[:], [pair[:, 0, :], pair[:, 1, :]])
                nc.scalar.activation(inverse[t][:, cols], spread[:], ACT.Abs_reciprocal_sqrt, bias=quarter[:])

        def numerator(t):
            nc.vector.scalar_tensor_tensor(top[t][:], h_neg[t][:], 1.32, both[t][:], ALU.mult, ALU.add)

        def finish(t, cols):
            result = ring.tile([P, cols.stop - cols.start], F32, name="result")
            nc.vector.scalar_tensor_tensor(result[:], top[t][:, cols], -0.3125, inverse[t][:, cols], ALU.mult, ALU.mult)
            nc.sync.dma_start(out=out_rows[:, t, cols], in_=result[:])

        fetch(0)
        fetch(1)
        numerator(0)
        fetch(2)
        finish(0, whole)
        numerator(1)
        fetch(3)
        numerator(2)
        finish(1, whole)
        numerator(3)
        finish(2, whole)
        finish(3, halves[0])
        finish(3, halves[1])
